import numpy as np, ml_dtypes
CORES = [16,32,48,64,80]
N = 5
V, K, ROUNDS = 4096, 4, 3
CAPP = 128
def entries(a): return a.T.reshape(-1)
def pack(v, P): return np.ascontiguousarray(np.asarray(v, np.int32).reshape(-1, P).T)
def lists(rng, how):
    T = V * K; me = np.arange(N)[:, None]
    O = np.broadcast_to(me, (N, T)).copy()
    for r in range(N):
        p = rng.permutation(T); a = 0
        if how == "clump": p = (CAPP * int(rng.integers(T // CAPP)) + np.arange(T)) % T
        if how == "clump" and r % 2: p = 16 * (p % (T // 16)) + p // (T // 16)
        for o in range(N):
            if o != r: c = CAPP if how in ("clump", "full") else int(rng.integers(0, CAPP + 1)); O[r, p[a:a + c]] = o; a += c
    I = V * O + rng.integers(0, V, (N, T))
    if how == "alike": I = V * O + rng.integers(0, V, N)[O]
    if how == "edge": I = V * O + np.where(rng.random((N, T)) < 0.5, 0, V - 1)
    if how == "line": I = np.minimum(V * me + np.arange(T)[None, :] // K + 1, N * V - 1)
    return {"nb": np.stack([pack(i, 16) for i in I])}
def setup_inputs(rng):
    return dict({"x": rng.standard_normal((N, 128, V), dtype=np.float32).astype(ml_dtypes.bfloat16)}, **lists(rng, "uniform"))
def setup_inputs_alike(rng):
    d = setup_inputs(rng); d.update(lists(rng, "alike"))
    for k in ("x",): d[k] = (d[k].astype(np.float32) * 1048576.0).astype(d[k].dtype)
    return d
def setup_inputs_clump(rng):
    d = setup_inputs(rng); d.update(lists(rng, "clump"))
    for k in ("x",): d[k] = (d[k].astype(np.float32) * (1 / 1024.0)).astype(d[k].dtype)
    return d
def setup_inputs_edge(rng):
    d = setup_inputs(rng); d.update(lists(rng, "edge"))
    return d
def setup_inputs_full(rng):
    d = setup_inputs(rng); d.update(lists(rng, "full"))
    return d
def setup_inputs_line(rng):
    d = setup_inputs(rng); d.update(lists(rng, "line"))
    return d
def check_inputs(x):
    bad = []
    if x["nb"].min() < 0 or x["nb"].max() >= N * V: bad.append("nb out of range")
    if np.abs(x["x"].astype(np.float32)).max() > 1e30: bad.append("x beyond -1e30 to 1e30")
    for r in range(N):
        c = np.bincount(entries(x["nb"][r]) // V, minlength=N); c[r] = 0
        if int(c.max()) > CAPP: bad.append("more than CAPP entries of a list point into one other rank's part")
    return bad
def reference(x, nb):
    A = np.concatenate(list(x), axis=1)
    NB = np.concatenate([entries(a) for a in nb]).reshape(N * V, K)
    for k in range(ROUNDS):
        B = A.copy()
        for j in range(K): B = np.maximum(B, A[:, NB[:, j]])
        A = B
    return {"y": np.stack([A[:, V * r:V * r + V] for r in range(N)])}

@@ -1,0 +1,361 @@
+from concourse.bass import DstId, RemoteDMATransfer
+from concourse.mybir import AluOpType, ActivationFunctionType
+
+A = AluOpType
+COPY = ActivationFunctionType.Copy
+ABS = ActivationFunctionType.Abs
+BF, F32, I32, U16 = "bfloat16", "float32", "int32", "uint16"
+SCRATCH = {
+    "NB": ("sbuf", [128, 128], I32), "XS": ("dram", [8, 128, 512], BF), "XL": ("sbuf", [128, 512], BF),
+    "YDA": ("dram", [8, 128, 256], BF), "YDB": ("dram", [8, 128, 256], BF), "Y": ("sbuf", [128, 512], BF),
+    "WIN": ("sbuf", [128, 4608], BF), "GA": ("sbuf", [128, 2048], BF), "SC": ("sbuf", [128, 2048], BF),
+    "GS": ("sbuf", [128, 512], BF), "REQ": ("sbuf", [128, 32], U16), "RQ": ("sbuf", [128, 32], U16),
+    "OFF": ("sbuf", [128, 128], U16), "SEL": ("sbuf", [128, 1024], BF), "BLK": ("sbuf", [128, 1024], BF),
+    "MK0": ("sbuf", [128, 1024], BF), "MK": ("sbuf", [128, 1024], BF),
+    "MS": ("sbuf", [128, 516], BF), "CC": ("sbuf", [128, 516], BF), "DD": ("sbuf", [128, 516], BF),
+    "PP": ("sbuf", [128, 516], BF), "SM": ("sbuf", [128, 516], BF),
+}
+for _k in range(3):
+    SCRATCH["OWN%d" % _k] = ("sbuf", [128, 528], BF)
+    SCRATCH["HS%d" % _k] = ("sbuf", [128, 64], BF)
+    SCRATCH["HL%d" % _k] = ("sbuf", [128, 64], BF)
+BANKS = ("R0", "R1", "R2", "R3", "OP", "PC", "PH", "LS")
+for _k in BANKS:
+    SCRATCH[_k] = ("psum", [128, 512], F32)
+TILE = {}
+for _b, _d, _l in (("TF", F32, "T16F 128 B8A 16 B8B 16 B8 16 SP1 16 GC 16 NS 16 RC 16 RD 32 HT 512 PR 512 JK 512 "
+                    "FA 128 FB 128 FC 128 FD 128 FE 128 FF 128 FG 128 RM 128"),
+                   ("TI", I32, "DK 128 DM 128 PI 16 PJ 16 OW 128 HI 128 LO 128 VL 128 W1 32 W2 32"),
+                   ("TB", BF, "ONE 128 T16 128 IDT 128 TRS 128 TRI 128 PRM 128 IOT 128 HB 128 LB 128 AB 512 EE 512")):
+    _l, _n = _l.split(), 0
+    for _i in range(0, len(_l), 2):
+        TILE[_l[_i]] = (_b, _n, int(_l[_i + 1]))
+        _n += int(_l[_i + 1])
+    SCRATCH[_b] = ("sbuf", [128, _n], _d)
+SEMAPHORES = ["cv", "cs", "ct", "cp", "nbl", "xll", "xfl", "xnl", "xar", "rar", "far", "oar", "h0", "h1", "h2", "yra", "yrb",
+              "loc", "yla", "ylb", "yo"]
+
+
+def tracker(g, T):
+    Q = {"v": g.vector, "s": g.scalar, "t": g.tensor, "p": g, "y": g.sync}
+    seen = {q: {} for q in Q}
+    last, reads, know, bank, total = {}, {}, {}, {}, {}
+
+    def wait(q, evs):
+        for sem, val in sorted(evs):
+            if seen[q].get(sem, 0) < val:
+                Q[q].wait_ge(T.sem[sem], val)
+                seen[q][sem] = val
+                for s2, v2 in know.get((sem, val), {}).items():
+                    if seen[q].get(s2, 0) < v2:
+                        seen[q][s2] = v2
+
+    def before(q, r, w, but=None):
+        top = {}
+
+        def add(e):
+            if e[0] != but and top.get(e[0], 0) < e[1]:
+                top[e[0]] = e[1]
+        for k in list(r) + list(w):
+            if k in BANKS:
+                for q2, e in bank.get(k, {}).items():
+                    if q2 != q:
+                        add(e)
+            elif k in last:
+                add(last[k])
+        for k in w:
+            if k not in BANKS:
+                for e in reads.get(k, []):
+                    add(e)
+        wait(q, top.items())
+
+    def after(q, r, w, e):
+        know[e] = dict(seen[q])
+        for k in list(r) + list(w):
+            if k in BANKS:
+                bank.setdefault(k, {})[q] = e
+            elif k in w:
+                last[k] = e
+                reads[k] = []
+            else:
+                reads.setdefault(k, []).append(e)
+
+    def op(q, r, w, name, *args, **kw):
+        r, w = r.split(), w.split()
+        before(q, r, w)
+        fn = {"copy": Q["v"].tensor_copy, "tt": Q["v"].tensor_tensor, "ts": Q["v"].tensor_scalar,
+              "scan": Q["v"].tensor_tensor_scan, "fill": Q["v"].memset, "act": Q["s"].activation,
+              "mm": Q["t"].matmul, "iota": g.iota, "sel": g.affine_select}[name]
+        sem = "c" + q
+        total[sem] = total.get(sem, 0) + 1
+        fn(*args, **kw).then_inc(T.sem[sem], 1)
+        after(q, r, w, (sem, total[sem]))
+
+    def dma(q, r, w, sem, out, in_, upto):
+        r, w = r.split(), w.split()
+        before(q, r, w, sem)
+        total[sem] = upto
+        Q[q].dma_start(out, in_).then_inc(T.sem[sem], 16)
+        after(q, r, w, (sem, upto))
+
+    def arrives(k, sem, n):
+        total[sem] = n
+        last[k] = (sem, n)
+
+    def send(r, transfers, n):
+        before("p", r.split(), [])
+        total["loc"] = total.get("loc", 0) + n
+        g.remote_dma_fused(transfers, local_sem=T.sem.loc)
+
+    def finish():
+        for sem in sorted(total):
+            wait("p", [(sem, total[sem])])
+    return op, dma, arrives, send, finish
+
+
+def rank_program(g, core, T, topo):
+    N = len(T.cores)
+    team = [[R] + [c for c in range(16 * 8) if topo.chip(c) == topo.chip(R) and c != R] for R in T.cores]
+    mine = [r for r in range(N) if core in team[r]]
+    if not mine:
+        return
+    r = mine[0]
+    me = team[r].index(core)
+    first = me == 0
+    others = [o for o in range(N) if o != r]
+    op, dma, arrives, send, finish = tracker(g, T)
+    bits = {}
+
+    def engines(dst):
+        if dst not in bits:
+            m = topo.mask(core, dst)
+            bits[dst] = [e for e in range(m.bit_length()) if m >> e & 1]
+        return bits[dst]
+
+    def transfer(dst, src_ap, dst_ap, eng, sem):
+        rid, pid = topo.addr(dst)[:2]
+        return RemoteDMATransfer(dst_ids=[DstId(rid=rid, pnc=pid)], dma_engine_mask=sum(1 << e for e in eng),
+                                 remote_sem=T.sem[sem], src=src_ap, dst=dst_ap)
+
+    far = [c for c in team[r][1:] if topo.die(c) != topo.die(core)]
+    near = [c for c in team[r][1:] if topo.die(c) == topo.die(core)]
+
+    def to_some(key, cs, n, src, dst, sem):
+        tr = [transfer(c, src(team[r].index(c)), dst, engines(c)[n * i:n * i + n], sem) for i, c in enumerate(cs)]
+        send(key, tr, n * len(tr))
+
+    def to_team(key, ap, sem):
+        tr = []
+        for half, cs in enumerate((far, near)):
+            for i, c in enumerate(cs):
+                tr.append(transfer(c, ap, ap, engines(c)[half::2][2 * i:2 * i + 2], sem))
+        send(key, tr, 2 * len(tr))
+
+    def to_ranks(key, src, dst, at, sem):
+        tr = []
+        for i, o in enumerate(others):
+            c = team[o][at]
+            j = [k for k in range(N) if k != o].index(r)
+            tr.append(transfer(c, src(i), dst(j), engines(c)[2 * i:2 * i + 2], sem))
+        send(key, tr, 2 * len(tr))
+
+    def V(n, a=0, b=None):
+        buf, c0, w = TILE[n]
+        return T[buf][:, c0 + a:c0 + (w if b is None else b)]
+
+    def col(n, i=0):
+        return V(n, i, i + 1)
+
+    def part(n, i):
+        return V(n, 128 * i, 128 * i + 128)
+
+    four = range(4)
+    if first:
+        for k in range(8):
+            dma("ys"[k % 2], "", "NB", "nbl", T.NB[16 * k:16 * k + 16, :], T.nb[:, 128 * k:128 * k + 128], 128)
+        nf, ne = [team[r].index(c) for c in far], [team[r].index(c) for c in near]
+        dma("y", "", "XSF", "xfl", T.XS[nf[0]:nf[-1] + 1], T.x[16 * nf[0]:16 * nf[-1] + 16, :], 16)
+        dma("s", "", "XSN", "xnl", T.XS[ne[0]:ne[-1] + 1], T.x[16 * ne[0]:16 * ne[-1] + 16, :], 16)
+        dma("s", "", "XL", "xll", T.XL[:, :], T.x[0:16, :], 16)
+        arrives("REQ", "rar", 2 * len(others))
+        arrives("YRA", "yra", 7 * 16)
+        arrives("YRB", "yrb", 7 * 16)
+    else:
+        arrives("XL", "xar", 4)
+        arrives("REQ", "far", 2)
+        arrives("OFF", "oar", 2)
+    for k in range(3):
+        arrives("HL%d" % k, "h%d" % k, 2 * len(others))
+
+    loose = dict(allow_small_or_imprecise_dtypes=True)
+    op("v", "", "ONE", "fill", V("ONE"), 1.0)
+    op("v", "", "B8A", "fill", V("B8A"), 1.0)
+    op("p", "", "DK", "iota", V("DK"), [[1, 128]], 128, -1)
+    op("p", "B8A", "B8B", "sel", V("B8B", 0, 8), V("B8A", 0, 8), [[-16, 8]], A.is_ge, 0.0, 0, 1)
+    op("p", "B8B", "B8", "sel", V("B8", 0, 8), V("B8B", 0, 8), [[16, 8]], A.is_ge, 0.0, 15, -1)
+    if first:
+        op("p", "", "PI", "iota", col("PI"), [[0, 1]], 0, 1)
+        op("p", "", "IOT", "iota", V("IOT"), [[2, 128]], 1, 0, **loose)
+        op("p", "", "SP1", "iota", col("SP1"), [[0, 1]], 1, 2, **loose)
+    op("p", "ONE", "PRM", "sel", V("PRM"), V("ONE"), [[-1, 8], [-8, 16]], A.is_equal, 0.0, 0, 1)
+    op("v", "DK", "DM", "ts", V("DM"), V("DK"), 15, None, A.bitwise_and)
+    if first:
+        op("v", "DK", "TRS", "ts", V("TRS"), V("DK"), 128.0, None, A.is_gt)
+        op("v", "DK", "TRI", "ts", V("TRI"), V("DK"), 128.0, None, A.is_ge)
+        op("v", "", "SM", "fill", T.SM[:, :], 1.0)
+        op("v", "", "MS", "fill", T.MS[:, :], 0.0)
+        op("v", "DM", "T16F", "ts", V("T16F"), V("DM"), 0.0, None, A.is_equal)
+        op("v", "PI", "PJ", "ts", col("PJ"), col("PI"), 4, None, A.logical_shift_right)
+        op("v", "", "SM", "fill", T.SM[:, 0:516:129], 0.0)
+        op("v", "PJ", "GC", "ts", col("GC"), col("PJ"), -512.0, None, A.mult)
+        to_some("XSF", far, 4, lambda c: T.XS[c], T.XL[:, :], "xar")
+        to_some("XSN", near, 4, lambda c: T.XS[c], T.XL[:, :], "xar")
+    op("v", "DM", "T16", "ts", V("T16"), V("DM"), 0.0, None, A.is_equal)
+    op("v", "DK", "IDT", "ts", V("IDT"), V("DK"), 128.0, None, A.is_equal)
+
+    def late_constants():
+        op("v", "", "BLK", "fill", T.BLK[:, :], 0.0)
+        for a in range(8):
+            op("v", "T16 B8", "SEL%d" % a, "ts", T.SEL[:, 128 * a:128 * a + 128], V("T16"), col("B8", a), None, A.mult)
+        for a in range(8):
+            op("v", "T16 BLK", "BLK%d" % a, "copy", T.BLK[:, 144 * a:144 * a + 16], V("T16", 16 * a, 16 * a + 16))
+        op("v", "", "MK0", "fill", T.MK0[:, :], 1e29)
+        for k in range(3):
+            op("v", "", "ZZ%d" % k, "fill", T["OWN%d" % k][:, 512:528], 0.0)
+        op("v", "", "MK0", "fill", T.MK0[:, 0:1024:4], -1e29)
+        op("v", "MK0", "MK", "ts", T.MK[:, :], T.MK0[:, :], 1e5, None, A.mult)
+
+    def all4(n):
+        return " ".join(n + str(i) for i in four)
+
+    def blk(t, o, k):
+        return t[:, 129 * o + k:129 * o + k + 128]
+    if first:
+        op("v", "NB", "OW", "ts", V("OW"), T.NB[:, :], 12, None, A.logical_shift_right)
+        op("v", "NB", "HI", "ts", V("HI"), T.NB[:, :], 4032, None, A.bitwise_and)
+        op("v", "NB", "LO", "ts", V("LO"), T.NB[:, :], 63, None, A.bitwise_and)
+        for i, o in enumerate(others):
+            op("v", "OW MS", "MS%d" % i, "ts", blk(T.MS, i, 1), V("OW"), float(o), None, A.is_equal)
+        op("v", "SM MS " + all4("MS"), "CC", "scan", T.CC[:, :], T.SM[:, :], T.MS[:, :], 0.0, A.mult, A.add)
+        tot = T.CC[:, 128:516:129]
+        op("t", "TRS CC", "LS", "mm", T.LS[:, 0:4], V("TRS"), tot, True, True)
+        op("t", "TRS CC", "LS", "mm", T.LS[:, 4:8], V("TRS"), tot, True, False)
+        op("t", "TRI CC", "LS", "mm", T.LS[:, 4:8], V("TRI"), tot, False, True)
+        op("v", "HI", "HB", "copy", V("HB"), V("HI"))
+        op("v", "LO", "LB", "copy", V("LB"), V("LO"))
+        op("v", "LS", "NS", "ts", V("NS", 0, 8), T.LS[:, 0:8], -1.0, None, A.mult)
+        for i in four:
+            op("s", "IOT NS", "AB%d" % i, "act", part("AB", i), V("IOT"), ABS, bias=col("NS", 4 + i))
+        for i in four:
+            op("v", "CC NS", "DD%d" % i, "ts", T.DD[:, 129 * i:129 * i + 129], T.CC[:, 129 * i:129 * i + 129], col("NS", i),
+               None, A.subtract)
+            op("v", "AB%d CC" % i, "EE%d" % i, "ts", part("EE", i), part("AB", i), T.CC[:, 129 * i + 128:129 * i + 129],
+               None, A.is_lt)
+        for i in four:
+            b, e = "R%d" % i, "EE%d " % i
+            E = part("EE", i)
+            op("t", e + "DD%d" % i, b, "mm", T[b][:, 0:128], E, blk(T.DD, i, 1), True, False)
+            op("t", e + "DD%d" % i, b, "mm", T[b][:, 0:128], E, blk(T.DD, i, 0), False, True)
+            op("t", e + "HB", b, "mm", T[b][:, 128:256], E, V("HB"), True, False)
+            op("t", e + "LB", b, "mm", T[b][:, 128:256], E, V("LB"), False, True)
+        for i in four:
+            b = "R%d" % i
+            op("v", b + " SP1", "HT%d" % i, "ts", part("HT", i), T[b][:, 0:128], col("SP1"), None, A.is_equal)
+            op("v", b + " HT%d" % i, "PR%d" % i, "tt", part("PR", i), part("HT", i), T[b][:, 128:256], A.mult)
+            op("s", "PR%d" % i, "RC%d JK%d" % (i, i), "act", part("JK", i), part("PR", i), COPY, accum_out=col("RC", i))
+        op("v", "OW", "FA", "ts", V("FA"), V("OW"), float(r), -128.0, A.is_gt, A.mult)
+        op("v", "OW", "FB", "ts", V("FB"), V("OW"), 128.0, 4095.0, A.mult, A.add)
+        for i in four:
+            op("v", "RC%d B8" % i, "RD%d" % i, "ts", V("RD", 8 * i, 8 * i + 8), V("B8", 0, 8), col("RC", i), None, A.mult)
+        op("t", "T16F " + all4("RD"), "LS", "mm", T.LS[:, 16:48], V("T16F"), V("RD"), True, True)
+        op("v", "FA FB", "FC", "tt", V("FC"), V("FA"), V("FB"), A.add)
+        op("v", "LS GC", "W1", "ts", V("W1"), T.LS[:, 16:48], col("GC"), None, A.add)
+        op("v", "W1", "W2", "ts", V("W2"), V("W1"), 4095, None, A.bitwise_and)
+        op("v", "W2", "RQ", "ts", T.RQ[:, :], V("W2"), 512.0, None, A.min)
+        to_ranks("RQ", lambda i: T.RQ[:, 8 * i:8 * i + 8], lambda j: T.REQ[:, 8 * j:8 * j + 8], 0, "rar")
+        op("v", "MS " + all4("MS") + " " + all4("DD"), "PP", "tt", T.PP[:, :], T.MS[:, :], T.DD[:, :], A.mult)
+        for i in four:
+            op("t", "IDT PP", "LS", "mm", T.LS[:, 128:256], V("IDT"), blk(T.PP, i, 1), i == 0, i == 3)
+        op("v", "OW", "RM", "ts", V("RM"), V("OW"), float(r), None, A.not_equal)
+        op("v", "NB", "VL", "ts", V("VL"), T.NB[:, :], 4095, None, A.bitwise_and)
+        op("v", "FC VL", "FE", "tt", V("FE"), V("FC"), V("VL"), A.subtract)
+        op("v", "FE LS", "FD", "tt", V("FD"), V("FE"), T.LS[:, 128:256], A.add)
+        op("v", "FD RM", "FF", "tt", V("FF"), V("FD"), V("RM"), A.mult)
+        op("v", "FF VL", "FG", "tt", V("FG"), V("FF"), V("VL"), A.add)
+        op("v", "FG", "OFF", "copy", T.OFF[:, :], V("FG"))
+        to_team("OFF", T.OFF[:, :], "oar")
+    late_constants()
+
+    def own(k):
+        return all4("OWN%d_" % k)
+
+    def sel(a):
+        return T.SEL[:, 128 * a:128 * a + 128]
+
+    def request(k):
+        win = T["OWN%d" % k][:, 0:528]
+        rk = "REQ ZZ%d " % k + own(k)
+        op("v", rk, "GS0", "copy", T.GS[:, 0:256], win.indirect(T.REQ[:, 0:16]))
+        op("s", rk, "GS1", "act", T.GS[:, 256:512], win.indirect(T.REQ[:, 16:32]), COPY)
+        for a in range(8):
+            op("t", "GS0 GS1 BLK%d" % a, "PC", "mm", T.PC[:, 0:64], T.BLK[:, 128 * a:128 * a + 128], T.GS[:, a:512:8],
+               a == 0, a == 7)
+        hs, hl = "HS%d" % k, "HL%d" % k
+        op("v", "PC", hs, "copy", T[hs][:, :], T.PC[:, 0:64])
+        to_ranks(hs, lambda i: T[hs][:, 16 * i:16 * i + 16], lambda j: T[hl][:, 16 * j:16 * j + 16], me, "h%d" % k)
+
+    def replicate(k, vec):
+        for a in range(8):
+            b = "R%d" % (a % 4)
+            op("t", own(k) + " SEL%d" % a, b, "mm", T[b][:, :], sel(a), T["OWN%d" % k][:, 0:512], True, True)
+            out = T.WIN[:, 512 * a:512 * a + 512]
+            if a in vec:
+                op("v", b, "WIN%d" % a, "copy", out, T[b][:, :])
+            else:
+                op("s", b, "WIN%d" % a, "act", out, T[b][:, :], COPY)
+
+    def sweep(k):
+        h = "HL%d" % k
+        for b, p in (("PH", 0), ("LS", 1)):
+            for a in range(p, 8, 2):
+                op("t", h + " SEL%d" % a, b, "mm", T[b][:, a // 2:256:4], sel(a), T[h][:, :], True, True)
+        op("v", "PH", "WIN8", "copy", T.WIN[:, 4096:4608:2], T.PH[:, 0:256])
+        op("s", "LS", "WIN9", "act", T.WIN[:, 4097:4608:2], T.LS[:, 0:256], COPY)
+        cut = [(0, 128), (128, 256), (256, 432), (432, 512)]
+        out = T["OWN%d" % (k + 1)] if k < 2 else T.Y
+        dst = (own(k + 1) if k < 2 else all4("Y")).split()
+        rk = "OFF WIN8 WIN9 " + all4("WIN") + " WIN4 WIN5 WIN6 WIN7"
+        for i, (a, b) in enumerate(cut):
+            nbr = T.WIN[:, 0:4608].indirect(T.OFF[:, a // 4:b // 4])
+            if i == 0:
+                op("v", rk, "GA0", "copy", T.GA[:, 4 * a:4 * b], nbr)
+            else:
+                op("s", rk, "GA%d" % i, "act", T.GA[:, 4 * a:4 * b], nbr, COPY)
+        for i, (a, b) in enumerate(cut):
+            op("v", "GA%d MK" % i, "SC%d" % i, "scan", T.SC[:, 4 * a:4 * b], T.MK[:, 0:4 * (b - a)], T.GA[:, 4 * a:4 * b],
+               0.0, A.min, A.max)
+            op("v", "OP SC%d" % i, dst[i], "tt", out[:, a:b], T.SC[:, 4 * a + 3:4 * b:4], T.OP[:, a:b], A.max)
+
+    op("t", "XL PRM", "OP", "mm", T.OP[:, :], V("PRM"), T.XL[:, :], True, True)
+    op("s", "OP", own(0), "act", T.OWN0[:, 0:512], T.OP[:, :], COPY)
+    if first:
+        to_team("REQ", T.REQ[:, :], "far")
+    for k in range(3):
+        request(k)
+        if k:
+            op("t", own(k) + " IDT", "OP", "mm", T.OP[:, :], V("IDT"), T["OWN%d" % k][:, 0:512], True, True)
+        replicate(k, (0, 2, 4, 6))
+        sweep(k)
+
+    for h, ks in (("A", "Y0 Y1"), ("B", "Y2 Y3")):
+        lo = 256 * (h == "B")
+        yd, s = T["YD" + h], h.lower()
+        if first:
+            dma("y", ks, "YD" + h, "yl" + s, yd[0], T.Y[:, lo:lo + 256], 16)
+            for k in range(8):
+                dma("ys"[k % 2], "YD%s YR%s" % (h, h), "y", "yo", T.y[:, 512 * k + lo:512 * k + lo + 256],
+                    yd[:, 16 * k:16 * k + 16, :], 256)
+        else:
+            e = engines(team[r][0])
+            send(ks, [transfer(team[r][0], T.Y[:, lo:lo + 256], yd[me], e, "yr" + s)], len(e))
+    finish()

@@ -5,13 +5,15 @@ A = AluOpType
 COPY = ActivationFunctionType.Copy
 ABS = ActivationFunctionType.Abs
 BF, F32, I32, U16 = "bfloat16", "float32", "int32", "uint16"
+CUT = [(0, 80), (80, 176), (176, 304), (304, 424), (424, 512)]
+HALF = 304
 SCRATCH = {
     "NB": ("sbuf", [128, 128], I32), "XS": ("dram", [8, 128, 512], BF), "XL": ("sbuf", [128, 512], BF),
-    "YDA": ("dram", [8, 128, 256], BF), "YDB": ("dram", [8, 128, 256], BF), "Y": ("sbuf", [128, 512], BF),
+    "YDA": ("dram", [8, 128, HALF], BF), "YDB": ("dram", [8, 128, 512 - HALF], BF), "Y": ("sbuf", [128, 512], BF),
     "WIN": ("sbuf", [128, 4608], BF), "GA": ("sbuf", [128, 2048], BF), "SC": ("sbuf", [128, 2048], BF),
     "GS": ("sbuf", [128, 512], BF), "REQ": ("sbuf", [128, 32], U16), "RQ": ("sbuf", [128, 32], U16),
-    "OFF": ("sbuf", [128, 128], U16), "SEL": ("sbuf", [128, 1024], BF), "BLK": ("sbuf", [128, 1024], BF),
-    "MK0": ("sbuf", [128, 1024], BF), "MK": ("sbuf", [128, 1024], BF),
+    "OFF": ("sbuf", [128, 128], U16), "KB": ("sbuf", [128, 2048], BF),
+    "ONE": ("sbuf", [128, 128], BF), "MK0": ("sbuf", [128, 512], BF), "MK": ("sbuf", [128, 512], BF),
     "MS": ("sbuf", [128, 516], BF), "CC": ("sbuf", [128, 516], BF), "DD": ("sbuf", [128, 516], BF),
     "PP": ("sbuf", [128, 516], BF), "SM": ("sbuf", [128, 516], BF),
 }
@@ -25,15 +27,15 @@ for _k in BANKS:
 TILE = {}
 for _b, _d, _l in (("TF", F32, "T16F 128 B8A 16 B8B 16 B8 16 SP1 16 GC 16 NS 16 RC 16 RD 32 HT 512 PR 512 JK 512 "
                     "FA 128 FB 128 FC 128 FD 128 FE 128 FF 128 FG 128 RM 128"),
-                   ("TI", I32, "DK 128 DM 128 PI 16 PJ 16 OW 128 HI 128 LO 128 VL 128 W1 32 W2 32"),
-                   ("TB", BF, "ONE 128 T16 128 IDT 128 TRS 128 TRI 128 PRM 128 IOT 128 HB 128 LB 128 AB 512 EE 512")):
+                   ("TI", I32, "DK 128 DM 128 PI 16 PJ 16 OW 128 HI 128 LO 128 VL 128"),
+                   ("TB", BF, "T16 128 IDT 128 TRS 128 TRI 128 PRM 128 IOT 128 HB 128 LB 128 AB 512 EE 512")):
     _l, _n = _l.split(), 0
     for _i in range(0, len(_l), 2):
         TILE[_l[_i]] = (_b, _n, int(_l[_i + 1]))
         _n += int(_l[_i + 1])
     SCRATCH[_b] = ("sbuf", [128, _n], _d)
-SEMAPHORES = ["cv", "cs", "ct", "cp", "nbl", "xll", "xfl", "xnl", "xar", "rar", "far", "oar", "h0", "h1", "h2", "yra", "yrb",
-              "loc", "yla", "ylb", "yo"]
+SEMAPHORES = ["cv", "cs", "ct", "cp", "nbl", "xll", "xal", "xfl", "xnl", "xar", "kar", "rar", "far", "oar", "h0", "h1", "h2",
+              "yra", "yrb", "loc", "yo"]
 
 
 def tracker(g, T):
@@ -140,8 +142,9 @@ def rank_program(g, core, T, topo):
     far = [c for c in team[r][1:] if topo.die(c) != topo.die(core)]
     near = [c for c in team[r][1:] if topo.die(c) == topo.die(core)]
 
-    def to_some(key, cs, n, src, dst, sem):
-        tr = [transfer(c, src(team[r].index(c)), dst, engines(c)[n * i:n * i + n], sem) for i, c in enumerate(cs)]
+    def x_to(key, cs, n, half):
+        tr = [transfer(c, T.XS[team[r].index(c)], T.XL[:, :], engines(c)[half::2][n * i:n * i + n], "xar")
+              for i, c in enumerate(cs)]
         send(key, tr, n * len(tr))
 
     def to_team(key, ap, sem):
@@ -169,27 +172,70 @@ def rank_program(g, core, T, topo):
     def part(n, i):
         return V(n, 128 * i, 128 * i + 128)
 
+    def sel(a):
+        return T.KB[:, 256 * a:256 * a + 128]
+
+    def blkm(a):
+        return T.KB[:, 256 * a + 128:256 * a + 256]
+
     four = range(4)
+
+    def names(n, k=4):
+        return " ".join(n + str(i) for i in range(k))
+
     if first:
         for k in range(8):
             dma("ys"[k % 2], "", "NB", "nbl", T.NB[16 * k:16 * k + 16, :], T.nb[:, 128 * k:128 * k + 128], 128)
         nf, ne = [team[r].index(c) for c in far], [team[r].index(c) for c in near]
-        dma("y", "", "XSF", "xfl", T.XS[nf[0]:nf[-1] + 1], T.x[16 * nf[0]:16 * nf[-1] + 16, :], 16)
-        dma("s", "", "XSN", "xnl", T.XS[ne[0]:ne[-1] + 1], T.x[16 * ne[0]:16 * ne[-1] + 16, :], 16)
-        dma("s", "", "XL", "xll", T.XL[:, :], T.x[0:16, :], 16)
+        for key, sem, lo, hi in (("XSA", "xal", ne[0], ne[0] + 1), ("XSF", "xfl", nf[0], nf[-1] + 1),
+                                 ("XSN", "xnl", ne[1], ne[-1] + 1)):
+            dma("y", "", key, sem, T.XS[lo:hi], T.x[16 * lo:16 * hi, :], 16)
+        dma("y", "", "XL", "xll", T.XL[:, :], T.x[0:16, :], 16)
         arrives("REQ", "rar", 2 * len(others))
+        for a in range(1, 8):
+            arrives("SEL%d" % a, "kar", 7 * 16)
+            arrives("BLK%d" % a, "kar", 7 * 16)
         arrives("YRA", "yra", 7 * 16)
         arrives("YRB", "yrb", 7 * 16)
     else:
-        arrives("XL", "xar", 4)
+        arrives("XL", "xar", 4 if topo.die(core) == topo.die(team[r][0]) else 2)
         arrives("REQ", "far", 2)
         arrives("OFF", "oar", 2)
     for k in range(3):
         arrives("HL%d" % k, "h%d" % k, 2 * len(others))
 
+    def t16(n):
+        op("v", "DM", n, "ts", V(n), V("DM"), 0.0, None, A.is_equal)
+
+    def dm():
+        op("v", "DK", "DM", "ts", V("DM"), V("DK"), 15, None, A.bitwise_and)
+
+    def idt():
+        op("v", "DK", "IDT", "ts", V("IDT"), V("DK"), 128.0, None, A.is_equal)
+
+    def pads(k):
+        op("v", "", "ZA%d" % k, "fill", T["OWN%d" % k][:, 0:8], 0.0)
+        op("v", "", "ZZ%d" % k, "fill", T["OWN%d" % k][:, 520:528], 0.0)
+
+    def matrices(blocks, width):
+        t16("T16")
+        op("v", "", "KB", "fill", T.KB[:, 0:width], 0.0)
+        for a in blocks:
+            op("v", "T16 B8 KB", "SEL%d" % a, "ts", sel(a), V("T16"), col("B8", a), None, A.mult)
+            op("v", "T16 KB", "BLK%d" % a, "copy", T.KB[:, 272 * a + 128:272 * a + 144], V("T16", 16 * a, 16 * a + 16))
+
+    def for_sweep():
+        op("v", "", "MK0", "fill", T.MK0[:, :], 1e29)
+        pads(1)
+        pads(2)
+        op("v", "", "MK0", "fill", T.MK0[:, 0:512:4], -1e29)
+        if not first:
+            idt()
+        op("v", "MK0", "MK", "ts", T.MK[:, :], T.MK0[:, :], 1e5, None, A.mult)
+
     loose = dict(allow_small_or_imprecise_dtypes=True)
-    op("v", "", "ONE", "fill", V("ONE"), 1.0)
     op("v", "", "B8A", "fill", V("B8A"), 1.0)
+    op("v", "", "ONE", "fill", T.ONE[:, :], 1.0)
     op("p", "", "DK", "iota", V("DK"), [[1, 128]], 128, -1)
     op("p", "B8A", "B8B", "sel", V("B8B", 0, 8), V("B8A", 0, 8), [[-16, 8]], A.is_ge, 0.0, 0, 1)
     op("p", "B8B", "B8", "sel", V("B8", 0, 8), V("B8B", 0, 8), [[16, 8]], A.is_ge, 0.0, 15, -1)
@@ -197,52 +243,37 @@ def rank_program(g, core, T, topo):
         op("p", "", "PI", "iota", col("PI"), [[0, 1]], 0, 1)
         op("p", "", "IOT", "iota", V("IOT"), [[2, 128]], 1, 0, **loose)
         op("p", "", "SP1", "iota", col("SP1"), [[0, 1]], 1, 2, **loose)
-    op("p", "ONE", "PRM", "sel", V("PRM"), V("ONE"), [[-1, 8], [-8, 16]], A.is_equal, 0.0, 0, 1)
-    op("v", "DK", "DM", "ts", V("DM"), V("DK"), 15, None, A.bitwise_and)
+    op("p", "ONE", "PRM", "sel", V("PRM"), T.ONE[:, :], [[-1, 8], [-8, 16]], A.is_equal, 0.0, 0, 1)
     if first:
         op("v", "DK", "TRS", "ts", V("TRS"), V("DK"), 128.0, None, A.is_gt)
         op("v", "DK", "TRI", "ts", V("TRI"), V("DK"), 128.0, None, A.is_ge)
         op("v", "", "SM", "fill", T.SM[:, :], 1.0)
         op("v", "", "MS", "fill", T.MS[:, :], 0.0)
-        op("v", "DM", "T16F", "ts", V("T16F"), V("DM"), 0.0, None, A.is_equal)
-        op("v", "PI", "PJ", "ts", col("PJ"), col("PI"), 4, None, A.logical_shift_right)
         op("v", "", "SM", "fill", T.SM[:, 0:516:129], 0.0)
-        op("v", "PJ", "GC", "ts", col("GC"), col("PJ"), -512.0, None, A.mult)
-        to_some("XSF", far, 4, lambda c: T.XS[c], T.XL[:, :], "xar")
-        to_some("XSN", near, 4, lambda c: T.XS[c], T.XL[:, :], "xar")
-    op("v", "DM", "T16", "ts", V("T16"), V("DM"), 0.0, None, A.is_equal)
-    op("v", "DK", "IDT", "ts", V("IDT"), V("DK"), 128.0, None, A.is_equal)
-
-    def late_constants():
-        op("v", "", "BLK", "fill", T.BLK[:, :], 0.0)
-        for a in range(8):
-            op("v", "T16 B8", "SEL%d" % a, "ts", T.SEL[:, 128 * a:128 * a + 128], V("T16"), col("B8", a), None, A.mult)
-        for a in range(8):
-            op("v", "T16 BLK", "BLK%d" % a, "copy", T.BLK[:, 144 * a:144 * a + 16], V("T16", 16 * a, 16 * a + 16))
-        op("v", "", "MK0", "fill", T.MK0[:, :], 1e29)
-        for k in range(3):
-            op("v", "", "ZZ%d" % k, "fill", T["OWN%d" % k][:, 512:528], 0.0)
-        op("v", "", "MK0", "fill", T.MK0[:, 0:1024:4], -1e29)
-        op("v", "MK0", "MK", "ts", T.MK[:, :], T.MK0[:, :], 1e5, None, A.mult)
-
-    def all4(n):
-        return " ".join(n + str(i) for i in four)
+        x_to("XSA", near[0:1], 4, 1)
+        x_to("XSF", far, 2, 0)
+    else:
+        dm()
+        matrices([me] + [a for a in range(8) if a != me], 2048)
+        e = engines(team[r][0])
+        ap = T.KB[:, 256 * me:256 * me + 256]
+        send("SEL%d BLK%d" % (me, me), [transfer(team[r][0], ap, ap, e, "kar")], len(e))
+        pads(0)
+        for_sweep()
 
     def blk(t, o, k):
         return t[:, 129 * o + k:129 * o + k + 128]
     if first:
         op("v", "NB", "OW", "ts", V("OW"), T.NB[:, :], 12, None, A.logical_shift_right)
-        op("v", "NB", "HI", "ts", V("HI"), T.NB[:, :], 4032, None, A.bitwise_and)
-        op("v", "NB", "LO", "ts", V("LO"), T.NB[:, :], 63, None, A.bitwise_and)
         for i, o in enumerate(others):
             op("v", "OW MS", "MS%d" % i, "ts", blk(T.MS, i, 1), V("OW"), float(o), None, A.is_equal)
-        op("v", "SM MS " + all4("MS"), "CC", "scan", T.CC[:, :], T.SM[:, :], T.MS[:, :], 0.0, A.mult, A.add)
+        op("v", "SM MS " + names("MS"), "CC", "scan", T.CC[:, :], T.SM[:, :], T.MS[:, :], 0.0, A.mult, A.add)
         tot = T.CC[:, 128:516:129]
         op("t", "TRS CC", "LS", "mm", T.LS[:, 0:4], V("TRS"), tot, True, True)
         op("t", "TRS CC", "LS", "mm", T.LS[:, 4:8], V("TRS"), tot, True, False)
         op("t", "TRI CC", "LS", "mm", T.LS[:, 4:8], V("TRI"), tot, False, True)
-        op("v", "HI", "HB", "copy", V("HB"), V("HI"))
-        op("v", "LO", "LB", "copy", V("LB"), V("LO"))
+        op("v", "NB", "HI", "ts", V("HI"), T.NB[:, :], 4032, None, A.bitwise_and)
+        op("v", "NB", "LO", "ts", V("LO"), T.NB[:, :], 63, None, A.bitwise_and)
         op("v", "LS", "NS", "ts", V("NS", 0, 8), T.LS[:, 0:8], -1.0, None, A.mult)
         for i in four:
             op("s", "IOT NS", "AB%d" % i, "act", part("AB", i), V("IOT"), ABS, bias=col("NS", 4 + i))
@@ -251,6 +282,9 @@ def rank_program(g, core, T, topo):
                None, A.subtract)
             op("v", "AB%d CC" % i, "EE%d" % i, "ts", part("EE", i), part("AB", i), T.CC[:, 129 * i + 128:129 * i + 129],
                None, A.is_lt)
+            if i == 0:
+                op("v", "HI", "HB", "copy", V("HB"), V("HI"))
+                op("v", "LO", "LB", "copy", V("LB"), V("LO"))
         for i in four:
             b, e = "R%d" % i, "EE%d " % i
             E = part("EE", i)
@@ -258,61 +292,91 @@ def rank_program(g, core, T, topo):
             op("t", e + "DD%d" % i, b, "mm", T[b][:, 0:128], E, blk(T.DD, i, 0), False, True)
             op("t", e + "HB", b, "mm", T[b][:, 128:256], E, V("HB"), True, False)
             op("t", e + "LB", b, "mm", T[b][:, 128:256], E, V("LB"), False, True)
-        for i in four:
+        dm()
+        op("v", "PI", "PJ", "ts", col("PJ"), col("PI"), 4, None, A.logical_shift_right)
+
+        def hit(i):
             b = "R%d" % i
             op("v", b + " SP1", "HT%d" % i, "ts", part("HT", i), T[b][:, 0:128], col("SP1"), None, A.is_equal)
+
+        def prod(i):
+            b = "R%d" % i
             op("v", b + " HT%d" % i, "PR%d" % i, "tt", part("PR", i), part("HT", i), T[b][:, 128:256], A.mult)
             op("s", "PR%d" % i, "RC%d JK%d" % (i, i), "act", part("JK", i), part("PR", i), COPY, accum_out=col("RC", i))
-        op("v", "OW", "FA", "ts", V("FA"), V("OW"), float(r), -128.0, A.is_gt, A.mult)
-        op("v", "OW", "FB", "ts", V("FB"), V("OW"), 128.0, 4095.0, A.mult, A.add)
-        for i in four:
-            op("v", "RC%d B8" % i, "RD%d" % i, "ts", V("RD", 8 * i, 8 * i + 8), V("B8", 0, 8), col("RC", i), None, A.mult)
-        op("t", "T16F " + all4("RD"), "LS", "mm", T.LS[:, 16:48], V("T16F"), V("RD"), True, True)
-        op("v", "FA FB", "FC", "tt", V("FC"), V("FA"), V("FB"), A.add)
-        op("v", "LS GC", "W1", "ts", V("W1"), T.LS[:, 16:48], col("GC"), None, A.add)
-        op("v", "W1", "W2", "ts", V("W2"), V("W1"), 4095, None, A.bitwise_and)
-        op("v", "W2", "RQ", "ts", T.RQ[:, :], V("W2"), 512.0, None, A.min)
+
+        def spot(i):
+            op("s", "RC%d B8" % i, "RD%d" % i, "act", V("RD", 8 * i, 8 * i + 8), V("B8", 0, 8), COPY, scale=col("RC", i))
+        hit(0)
+        op("v", "PJ", "GC", "ts", col("GC"), col("PJ"), -512.0, 8.0, A.mult, A.add)
+        prod(0)
+        hit(1)
+        t16("T16F")
+        prod(1)
+        hit(2)
+        spot(0)
+        prod(2)
+        hit(3)
+        spot(1)
+        prod(3)
+        spot(2)
+        spot(3)
+        op("t", "T16F " + names("RD"), "LS", "mm", T.LS[:, 16:48], V("T16F"), V("RD"), True, True)
+        op("v", "LS GC", "RQ", "ts", T.RQ[:, :], T.LS[:, 16:48], col("GC"), 520.0, A.add, A.min)
         to_ranks("RQ", lambda i: T.RQ[:, 8 * i:8 * i + 8], lambda j: T.REQ[:, 8 * j:8 * j + 8], 0, "rar")
-        op("v", "MS " + all4("MS") + " " + all4("DD"), "PP", "tt", T.PP[:, :], T.MS[:, :], T.DD[:, :], A.mult)
+        x_to("XSN", near[1:], 4, 1)
+        op("v", "MS " + names("MS") + " " + names("DD"), "PP", "tt", T.PP[:, :], T.MS[:, :], T.DD[:, :], A.mult)
+        idt()
         for i in four:
             op("t", "IDT PP", "LS", "mm", T.LS[:, 128:256], V("IDT"), blk(T.PP, i, 1), i == 0, i == 3)
-        op("v", "OW", "RM", "ts", V("RM"), V("OW"), float(r), None, A.not_equal)
+        op("v", "OW", "FA", "ts", V("FA"), V("OW"), float(r), -128.0, A.is_gt, A.mult)
+        op("v", "OW", "FB", "ts", V("FB"), V("OW"), 128.0, 4095.0, A.mult, A.add)
         op("v", "NB", "VL", "ts", V("VL"), T.NB[:, :], 4095, None, A.bitwise_and)
+        op("v", "FA FB", "FC", "tt", V("FC"), V("FA"), V("FB"), A.add)
+        op("v", "OW", "RM", "ts", V("RM"), V("OW"), float(r), None, A.not_equal)
         op("v", "FC VL", "FE", "tt", V("FE"), V("FC"), V("VL"), A.subtract)
         op("v", "FE LS", "FD", "tt", V("FD"), V("FE"), T.LS[:, 128:256], A.add)
         op("v", "FD RM", "FF", "tt", V("FF"), V("FD"), V("RM"), A.mult)
         op("v", "FF VL", "FG", "tt", V("FG"), V("FF"), V("VL"), A.add)
         op("v", "FG", "OFF", "copy", T.OFF[:, :], V("FG"))
+        to_team("REQ", T.REQ[:, :], "far")
         to_team("OFF", T.OFF[:, :], "oar")
-    late_constants()
+        matrices([0], 256)
+        pads(0)
+
+    OPB = ("OP", "PC", "OP")
 
     def own(k):
-        return all4("OWN%d_" % k)
-
-    def sel(a):
-        return T.SEL[:, 128 * a:128 * a + 128]
+        return names("OWN%d_" % k, 5)
 
     def request(k):
         win = T["OWN%d" % k][:, 0:528]
-        rk = "REQ ZZ%d " % k + own(k)
+        rk = "REQ ZA%d ZZ%d " % (k, k) + own(k)
         op("v", rk, "GS0", "copy", T.GS[:, 0:256], win.indirect(T.REQ[:, 0:16]))
         op("s", rk, "GS1", "act", T.GS[:, 256:512], win.indirect(T.REQ[:, 16:32]), COPY)
         for a in range(8):
-            op("t", "GS0 GS1 BLK%d" % a, "PC", "mm", T.PC[:, 0:64], T.BLK[:, 128 * a:128 * a + 128], T.GS[:, a:512:8],
-               a == 0, a == 7)
+            op("t", "GS0 GS1 BLK%d" % a, "PH", "mm", T.PH[:, 0:64], blkm(a), T.GS[:, a:512:8], a == 0, a == 7)
         hs, hl = "HS%d" % k, "HL%d" % k
-        op("v", "PC", hs, "copy", T[hs][:, :], T.PC[:, 0:64])
+        op("v", "PH", hs, "copy", T[hs][:, :], T.PH[:, 0:64])
         to_ranks(hs, lambda i: T[hs][:, 16 * i:16 * i + 16], lambda j: T[hl][:, 16 * j:16 * j + 16], me, "h%d" % k)
 
-    def replicate(k, vec):
+    def spread(k, a, lo, hi, keys):
+        b = "R%d" % (a % 4)
+        op("t", keys + " SEL%d" % a, b, "mm", T[b][:, lo:hi], sel(a), T["OWN%d" % k][:, 8 + lo:8 + hi], True, True)
+
+    def own_psum(k, lo, hi, keys):
+        op("t", keys + " IDT", OPB[k], "mm", T[OPB[k]][:, lo:hi], V("IDT"), T["OWN%d" % k][:, 8 + lo:8 + hi], True, True)
+
+    def replicate(k):
+        if k:
+            own_psum(k, HALF, 512, own(k))
         for a in range(8):
             b = "R%d" % (a % 4)
-            op("t", own(k) + " SEL%d" % a, b, "mm", T[b][:, :], sel(a), T["OWN%d" % k][:, 0:512], True, True)
+            spread(k, a, HALF if k and a < 4 else 0, 512, own(k))
             out = T.WIN[:, 512 * a:512 * a + 512]
-            if a in vec:
-                op("v", b, "WIN%d" % a, "copy", out, T[b][:, :])
-            else:
+            if a % 2:
                 op("s", b, "WIN%d" % a, "act", out, T[b][:, :], COPY)
+            else:
+                op("v", b, "WIN%d" % a, "copy", out, T[b][:, :])
 
     def sweep(k):
         h = "HL%d" % k
@@ -321,41 +385,57 @@ def rank_program(g, core, T, topo):
                 op("t", h + " SEL%d" % a, b, "mm", T[b][:, a // 2:256:4], sel(a), T[h][:, :], True, True)
         op("v", "PH", "WIN8", "copy", T.WIN[:, 4096:4608:2], T.PH[:, 0:256])
         op("s", "LS", "WIN9", "act", T.WIN[:, 4097:4608:2], T.LS[:, 0:256], COPY)
-        cut = [(0, 128), (128, 256), (256, 432), (432, 512)]
-        out = T["OWN%d" % (k + 1)] if k < 2 else T.Y
-        dst = (own(k + 1) if k < 2 else all4("Y")).split()
-        rk = "OFF WIN8 WIN9 " + all4("WIN") + " WIN4 WIN5 WIN6 WIN7"
-        for i, (a, b) in enumerate(cut):
+        out, o8 = (T["OWN%d" % (k + 1)], 8) if k < 2 else (T.Y, 0)
+        dst = own(k + 1).split() if k < 2 else names("Y", 5).split()
+        for i, (a, b) in enumerate(CUT):
             nbr = T.WIN[:, 0:4608].indirect(T.OFF[:, a // 4:b // 4])
             if i == 0:
-                op("v", rk, "GA0", "copy", T.GA[:, 4 * a:4 * b], nbr)
+                op("v", "OFF " + names("WIN", 10), "GA0", "copy", T.GA[:, 4 * a:4 * b], nbr)
             else:
-                op("s", rk, "GA%d" % i, "act", T.GA[:, 4 * a:4 * b], nbr, COPY)
-        for i, (a, b) in enumerate(cut):
+                op("s", "OFF " + names("WIN", 10), "GA%d" % i, "act", T.GA[:, 4 * a:4 * b], nbr, COPY)
+
+        def scan(i):
+            a, b = CUT[i]
             op("v", "GA%d MK" % i, "SC%d" % i, "scan", T.SC[:, 4 * a:4 * b], T.MK[:, 0:4 * (b - a)], T.GA[:, 4 * a:4 * b],
                0.0, A.min, A.max)
-            op("v", "OP SC%d" % i, dst[i], "tt", out[:, a:b], T.SC[:, 4 * a + 3:4 * b:4], T.OP[:, a:b], A.max)
 
+        def final(i):
+            a, b = CUT[i]
+            op("v", OPB[k] + " SC%d" % i, dst[i], "tt", out[:, o8 + a:o8 + b], T.SC[:, 4 * a + 3:4 * b:4], T[OPB[k]][:, a:b],
+               A.max)
+        for f, i in ((scan, 0), (scan, 1), (final, 0), (final, 1), (scan, 2), (final, 2), (scan, 3), (final, 3), (scan, 4),
+                     (final, 4)):
+            f(i)
+        if k < 2:
+            for a in four:
+                spread(k + 1, a, 0, HALF, " ".join(dst[0:3]))
+            own_psum(k + 1, 0, HALF, " ".join(dst[0:3]))
+
+    op("t", "XL PRM", "R0", "mm", T.R0[:, 0:256], V("PRM"), T.XL[:, 0:256], True, True)
+    op("t", "XL PRM", "R1", "mm", T.R1[:, 0:256], V("PRM"), T.XL[:, 256:512], True, True)
     op("t", "XL PRM", "OP", "mm", T.OP[:, :], V("PRM"), T.XL[:, :], True, True)
-    op("s", "OP", own(0), "act", T.OWN0[:, 0:512], T.OP[:, :], COPY)
     if first:
-        to_team("REQ", T.REQ[:, :], "far")
+        op("s", "R0", "OWN0_0 OWN0_1", "act", T.OWN0[:, 8:264], T.R0[:, 0:256], COPY)
+    else:
+        op("v", "R0", "OWN0_0 OWN0_1", "copy", T.OWN0[:, 8:264], T.R0[:, 0:256])
+    op("s", "R1", "OWN0_2 OWN0_3 OWN0_4", "act", T.OWN0[:, 264:520], T.R1[:, 0:256], COPY)
     for k in range(3):
         request(k)
-        if k:
-            op("t", own(k) + " IDT", "OP", "mm", T.OP[:, :], V("IDT"), T["OWN%d" % k][:, 0:512], True, True)
-        replicate(k, (0, 2, 4, 6))
+        if k == 0 and first:
+            for_sweep()
+        replicate(k)
         sweep(k)
 
-    for h, ks in (("A", "Y0 Y1"), ("B", "Y2 Y3")):
-        lo = 256 * (h == "B")
+    for h, ks, lo, hi in (("A", "Y0 Y1 Y2", 0, HALF), ("B", "Y3 Y4", HALF, 512)):
         yd, s = T["YD" + h], h.lower()
         if first:
-            dma("y", ks, "YD" + h, "yl" + s, yd[0], T.Y[:, lo:lo + 256], 16)
             for k in range(8):
-                dma("ys"[k % 2], "YD%s YR%s" % (h, h), "y", "yo", T.y[:, 512 * k + lo:512 * k + lo + 256],
-                    yd[:, 16 * k:16 * k + 16, :], 256)
+                dma("y" if h == "A" else "ys"[k % 2], ks, "y", "yo", T.y[0:16, 512 * k + lo:512 * k + hi],
+                    T.Y[16 * k:16 * k + 16, lo:hi], 512)
+            for k in range(8):
+                dma("ys"[k % 2], "YR" + h, "y", "yo", T.y[16:128, 512 * k + lo:512 * k + hi],
+                    yd[1:8, 16 * k:16 * k + 16, :], 512)
         else:
             e = engines(team[r][0])
-            send(ks, [transfer(team[r][0], T.Y[:, lo:lo + 256], yd[me], e, "yr" + s)], len(e))
+            send(ks, [transfer(team[r][0], T.Y[:, lo:hi], yd[me], e, "yr" + s)], len(e))
     finish()

from concourse.bass import DstId, RemoteDMATransfer
from concourse.mybir import AluOpType, ActivationFunctionType

A = AluOpType
COPY = ActivationFunctionType.Copy
ABS = ActivationFunctionType.Abs
BF, F32, I32, U16 = "bfloat16", "float32", "int32", "uint16"
CUT = [(0, 80), (80, 176), (176, 304), (304, 424), (424, 512)]
HALF = 304
SCRATCH = {
    "NB": ("sbuf", [128, 128], I32), "XS": ("dram", [8, 128, 512], BF), "XL": ("sbuf", [128, 512], BF),
    "YDA": ("dram", [8, 128, HALF], BF), "YDB": ("dram", [8, 128, 512 - HALF], BF), "Y": ("sbuf", [128, 512], BF),
    "WIN": ("sbuf", [128, 4608], BF), "GA": ("sbuf", [128, 2048], BF), "SC": ("sbuf", [128, 2048], BF),
    "GS": ("sbuf", [128, 512], BF), "REQ": ("sbuf", [128, 32], U16), "RQ": ("sbuf", [128, 32], U16),
    "OFF": ("sbuf", [128, 128], U16), "KB": ("sbuf", [128, 2048], BF),
    "ONE": ("sbuf", [128, 128], BF), "MK0": ("sbuf", [128, 512], BF), "MK": ("sbuf", [128, 512], BF),
    "MS": ("sbuf", [128, 516], BF), "CC": ("sbuf", [128, 516], BF), "DD": ("sbuf", [128, 516], BF),
    "PP": ("sbuf", [128, 516], BF), "SM": ("sbuf", [128, 516], BF),
}
for _k in range(3):
    SCRATCH["OWN%d" % _k] = ("sbuf", [128, 528], BF)
    SCRATCH["HS%d" % _k] = ("sbuf", [128, 64], BF)
    SCRATCH["HL%d" % _k] = ("sbuf", [128, 64], BF)
BANKS = ("R0", "R1", "R2", "R3", "OP", "PC", "PH", "LS")
for _k in BANKS:
    SCRATCH[_k] = ("psum", [128, 512], F32)
TILE = {}
for _b, _d, _l in (("TF", F32, "T16F 128 B8A 16 B8B 16 B8 16 SP1 16 GC 16 NS 16 RC 16 RD 32 HT 512 PR 512 JK 512 "
                    "FA 128 FB 128 FC 128 FD 128 FE 128 FF 128 FG 128 RM 128"),
                   ("TI", I32, "DK 128 DM 128 PI 16 PJ 16 OW 128 HI 128 LO 128 VL 128"),
                   ("TB", BF, "T16 128 IDT 128 TRS 128 TRI 128 PRM 128 IOT 128 HB 128 LB 128 AB 512 EE 512")):
    _l, _n = _l.split(), 0
    for _i in range(0, len(_l), 2):
        TILE[_l[_i]] = (_b, _n, int(_l[_i + 1]))
        _n += int(_l[_i + 1])
    SCRATCH[_b] = ("sbuf", [128, _n], _d)
SEMAPHORES = ["cv", "cs", "ct", "cp", "nbl", "xll", "xal", "xfl", "xnl", "xar", "kar", "rar", "far", "oar", "h0", "h1", "h2",
              "yra", "yrb", "loc", "yo"]


def tracker(g, T):
    Q = {"v": g.vector, "s": g.scalar, "t": g.tensor, "p": g, "y": g.sync}
    seen = {q: {} for q in Q}
    last, reads, know, bank, total = {}, {}, {}, {}, {}

    def wait(q, evs):
        for sem, val in sorted(evs):
            if seen[q].get(sem, 0) < val:
                Q[q].wait_ge(T.sem[sem], val)
                seen[q][sem] = val
                for s2, v2 in know.get((sem, val), {}).items():
                    if seen[q].get(s2, 0) < v2:
                        seen[q][s2] = v2

    def before(q, r, w, but=None):
        top = {}

        def add(e):
            if e[0] != but and top.get(e[0], 0) < e[1]:
                top[e[0]] = e[1]
        for k in list(r) + list(w):
            if k in BANKS:
                for q2, e in bank.get(k, {}).items():
                    if q2 != q:
                        add(e)
            elif k in last:
                add(last[k])
        for k in w:
            if k not in BANKS:
                for e in reads.get(k, []):
                    add(e)
        wait(q, top.items())

    def after(q, r, w, e):
        know[e] = dict(seen[q])
        for k in list(r) + list(w):
            if k in BANKS:
                bank.setdefault(k, {})[q] = e
            elif k in w:
                last[k] = e
                reads[k] = []
            else:
                reads.setdefault(k, []).append(e)

    def op(q, r, w, name, *args, **kw):
        r, w = r.split(), w.split()
        before(q, r, w)
        fn = {"copy": Q["v"].tensor_copy, "tt": Q["v"].tensor_tensor, "ts": Q["v"].tensor_scalar,
              "scan": Q["v"].tensor_tensor_scan, "fill": Q["v"].memset, "act": Q["s"].activation,
              "mm": Q["t"].matmul, "iota": g.iota, "sel": g.affine_select}[name]
        sem = "c" + q
        total[sem] = total.get(sem, 0) + 1
        fn(*args, **kw).then_inc(T.sem[sem], 1)
        after(q, r, w, (sem, total[sem]))

    def dma(q, r, w, sem, out, in_, upto):
        r, w = r.split(), w.split()
        before(q, r, w, sem)
        total[sem] = upto
        Q[q].dma_start(out, in_).then_inc(T.sem[sem], 16)
        after(q, r, w, (sem, upto))

    def arrives(k, sem, n):
        total[sem] = n
        last[k] = (sem, n)

    def send(r, transfers, n):
        before("p", r.split(), [])
        total["loc"] = total.get("loc", 0) + n
        g.remote_dma_fused(transfers, local_sem=T.sem.loc)

    def finish():
        for sem in sorted(total):
            wait("p", [(sem, total[sem])])
    return op, dma, arrives, send, finish


def rank_program(g, core, T, topo):
    N = len(T.cores)
    team = [[R] + [c for c in range(16 * 8) if topo.chip(c) == topo.chip(R) and c != R] for R in T.cores]
    mine = [r for r in range(N) if core in team[r]]
    if not mine:
        return
    r = mine[0]
    me = team[r].index(core)
    first = me == 0
    others = [o for o in range(N) if o != r]
    op, dma, arrives, send, finish = tracker(g, T)
    bits = {}

    def engines(dst):
        if dst not in bits:
            m = topo.mask(core, dst)
            bits[dst] = [e for e in range(m.bit_length()) if m >> e & 1]
        return bits[dst]

    def transfer(dst, src_ap, dst_ap, eng, sem):
        rid, pid = topo.addr(dst)[:2]
        return RemoteDMATransfer(dst_ids=[DstId(rid=rid, pnc=pid)], dma_engine_mask=sum(1 << e for e in eng),
                                 remote_sem=T.sem[sem], src=src_ap, dst=dst_ap)

    far = [c for c in team[r][1:] if topo.die(c) != topo.die(core)]
    near = [c for c in team[r][1:] if topo.die(c) == topo.die(core)]

    def x_to(key, cs, n, half):
        tr = [transfer(c, T.XS[team[r].index(c)], T.XL[:, :], engines(c)[half::2][n * i:n * i + n], "xar")
              for i, c in enumerate(cs)]
        send(key, tr, n * len(tr))

    def to_team(key, ap, sem):
        tr = []
        for half, cs in enumerate((far, near)):
            for i, c in enumerate(cs):
                tr.append(transfer(c, ap, ap, engines(c)[half::2][2 * i:2 * i + 2], sem))
        send(key, tr, 2 * len(tr))

    def to_ranks(key, src, dst, at, sem):
        tr = []
        for i, o in enumerate(others):
            c = team[o][at]
            j = [k for k in range(N) if k != o].index(r)
            tr.append(transfer(c, src(i), dst(j), engines(c)[2 * i:2 * i + 2], sem))
        send(key, tr, 2 * len(tr))

    def V(n, a=0, b=None):
        buf, c0, w = TILE[n]
        return T[buf][:, c0 + a:c0 + (w if b is None else b)]

    def col(n, i=0):
        return V(n, i, i + 1)

    def part(n, i):
        return V(n, 128 * i, 128 * i + 128)

    def sel(a):
        return T.KB[:, 256 * a:256 * a + 128]

    def blkm(a):
        return T.KB[:, 256 * a + 128:256 * a + 256]

    four = range(4)

    def names(n, k=4):
        return " ".join(n + str(i) for i in range(k))

    if first:
        for k in range(8):
            dma("ys"[k % 2], "", "NB", "nbl", T.NB[16 * k:16 * k + 16, :], T.nb[:, 128 * k:128 * k + 128], 128)
        nf, ne = [team[r].index(c) for c in far], [team[r].index(c) for c in near]
        for key, sem, lo, hi in (("XSA", "xal", ne[0], ne[0] + 1), ("XSF", "xfl", nf[0], nf[-1] + 1),
                                 ("XSN", "xnl", ne[1], ne[-1] + 1)):
            dma("y", "", key, sem, T.XS[lo:hi], T.x[16 * lo:16 * hi, :], 16)
        dma("y", "", "XL", "xll", T.XL[:, :], T.x[0:16, :], 16)
        arrives("REQ", "rar", 2 * len(others))
        for a in range(1, 8):
            arrives("SEL%d" % a, "kar", 7 * 16)
            arrives("BLK%d" % a, "kar", 7 * 16)
        arrives("YRA", "yra", 7 * 16)
        arrives("YRB", "yrb", 7 * 16)
    else:
        arrives("XL", "xar", 4 if topo.die(core) == topo.die(team[r][0]) else 2)
        arrives("REQ", "far", 2)
        arrives("OFF", "oar", 2)
    for k in range(3):
        arrives("HL%d" % k, "h%d" % k, 2 * len(others))

    def t16(n):
        op("v", "DM", n, "ts", V(n), V("DM"), 0.0, None, A.is_equal)

    def dm():
        op("v", "DK", "DM", "ts", V("DM"), V("DK"), 15, None, A.bitwise_and)

    def idt():
        op("v", "DK", "IDT", "ts", V("IDT"), V("DK"), 128.0, None, A.is_equal)

    def pads(k):
        op("v", "", "ZA%d" % k, "fill", T["OWN%d" % k][:, 0:8], 0.0)
        op("v", "", "ZZ%d" % k, "fill", T["OWN%d" % k][:, 520:528], 0.0)

    def matrices(blocks, width):
        t16("T16")
        op("v", "", "KB", "fill", T.KB[:, 0:width], 0.0)
        for a in blocks:
            op("v", "T16 B8 KB", "SEL%d" % a, "ts", sel(a), V("T16"), col("B8", a), None, A.mult)
            op("v", "T16 KB", "BLK%d" % a, "copy", T.KB[:, 272 * a + 128:272 * a + 144], V("T16", 16 * a, 16 * a + 16))

    def for_sweep():
        op("v", "", "MK0", "fill", T.MK0[:, :], 1e29)
        pads(1)
        pads(2)
        op("v", "", "MK0", "fill", T.MK0[:, 0:512:4], -1e29)
        if not first:
            idt()
        op("v", "MK0", "MK", "ts", T.MK[:, :], T.MK0[:, :], 1e5, None, A.mult)

    loose = dict(allow_small_or_imprecise_dtypes=True)
    op("v", "", "B8A", "fill", V("B8A"), 1.0)
    op("v", "", "ONE", "fill", T.ONE[:, :], 1.0)
    op("p", "", "DK", "iota", V("DK"), [[1, 128]], 128, -1)
    op("p", "B8A", "B8B", "sel", V("B8B", 0, 8), V("B8A", 0, 8), [[-16, 8]], A.is_ge, 0.0, 0, 1)
    op("p", "B8B", "B8", "sel", V("B8", 0, 8), V("B8B", 0, 8), [[16, 8]], A.is_ge, 0.0, 15, -1)
    if first:
        op("p", "", "PI", "iota", col("PI"), [[0, 1]], 0, 1)
        op("p", "", "IOT", "iota", V("IOT"), [[2, 128]], 1, 0, **loose)
        op("p", "", "SP1", "iota", col("SP1"), [[0, 1]], 1, 2, **loose)
    op("p", "ONE", "PRM", "sel", V("PRM"), T.ONE[:, :], [[-1, 8], [-8, 16]], A.is_equal, 0.0, 0, 1)
    if first:
        op("v", "DK", "TRS", "ts", V("TRS"), V("DK"), 128.0, None, A.is_gt)
        op("v", "DK", "TRI", "ts", V("TRI"), V("DK"), 128.0, None, A.is_ge)
        op("v", "", "SM", "fill", T.SM[:, :], 1.0)
        op("v", "", "MS", "fill", T.MS[:, :], 0.0)
        op("v", "", "SM", "fill", T.SM[:, 0:516:129], 0.0)
        x_to("XSA", near[0:1], 4, 1)
        x_to("XSF", far, 2, 0)
    else:
        dm()
        matrices([me] + [a for a in range(8) if a != me], 2048)
        e = engines(team[r][0])
        ap = T.KB[:, 256 * me:256 * me + 256]
        send("SEL%d BLK%d" % (me, me), [transfer(team[r][0], ap, ap, e, "kar")], len(e))
        pads(0)
        for_sweep()

    def blk(t, o, k):
        return t[:, 129 * o + k:129 * o + k + 128]
    if first:
        op("v", "NB", "OW", "ts", V("OW"), T.NB[:, :], 12, None, A.logical_shift_right)
        for i, o in enumerate(others):
            op("v", "OW MS", "MS%d" % i, "ts", blk(T.MS, i, 1), V("OW"), float(o), None, A.is_equal)
        op("v", "SM MS " + names("MS"), "CC", "scan", T.CC[:, :], T.SM[:, :], T.MS[:, :], 0.0, A.mult, A.add)
        tot = T.CC[:, 128:516:129]
        op("t", "TRS CC", "LS", "mm", T.LS[:, 0:4], V("TRS"), tot, True, True)
        op("t", "TRS CC", "LS", "mm", T.LS[:, 4:8], V("TRS"), tot, True, False)
        op("t", "TRI CC", "LS", "mm", T.LS[:, 4:8], V("TRI"), tot, False, True)
        op("v", "NB", "HI", "ts", V("HI"), T.NB[:, :], 4032, None, A.bitwise_and)
        op("v", "NB", "LO", "ts", V("LO"), T.NB[:, :], 63, None, A.bitwise_and)
        op("v", "LS", "NS", "ts", V("NS", 0, 8), T.LS[:, 0:8], -1.0, None, A.mult)
        for i in four:
            op("s", "IOT NS", "AB%d" % i, "act", part("AB", i), V("IOT"), ABS, bias=col("NS", 4 + i))
        for i in four:
            op("v", "CC NS", "DD%d" % i, "ts", T.DD[:, 129 * i:129 * i + 129], T.CC[:, 129 * i:129 * i + 129], col("NS", i),
               None, A.subtract)
            op("v", "AB%d CC" % i, "EE%d" % i, "ts", part("EE", i), part("AB", i), T.CC[:, 129 * i + 128:129 * i + 129],
               None, A.is_lt)
            if i == 0:
                op("v", "HI", "HB", "copy", V("HB"), V("HI"))
                op("v", "LO", "LB", "copy", V("LB"), V("LO"))
        for i in four:
            b, e = "R%d" % i, "EE%d " % i
            E = part("EE", i)
            op("t", e + "DD%d" % i, b, "mm", T[b][:, 0:128], E, blk(T.DD, i, 1), True, False)
            op("t", e + "DD%d" % i, b, "mm", T[b][:, 0:128], E, blk(T.DD, i, 0), False, True)
            op("t", e + "HB", b, "mm", T[b][:, 128:256], E, V("HB"), True, False)
            op("t", e + "LB", b, "mm", T[b][:, 128:256], E, V("LB"), False, True)
        dm()
        op("v", "PI", "PJ", "ts", col("PJ"), col("PI"), 4, None, A.logical_shift_right)

        def hit(i):
            b = "R%d" % i
            op("v", b + " SP1", "HT%d" % i, "ts", part("HT", i), T[b][:, 0:128], col("SP1"), None, A.is_equal)

        def prod(i):
            b = "R%d" % i
            op("v", b + " HT%d" % i, "PR%d" % i, "tt", part("PR", i), part("HT", i), T[b][:, 128:256], A.mult)
            op("s", "PR%d" % i, "RC%d JK%d" % (i, i), "act", part("JK", i), part("PR", i), COPY, accum_out=col("RC", i))

        def spot(i):
            op("s", "RC%d B8" % i, "RD%d" % i, "act", V("RD", 8 * i, 8 * i + 8), V("B8", 0, 8), COPY, scale=col("RC", i))
        hit(0)
        op("v", "PJ", "GC", "ts", col("GC"), col("PJ"), -512.0, 8.0, A.mult, A.add)
        prod(0)
        hit(1)
        t16("T16F")
        prod(1)
        hit(2)
        spot(0)
        prod(2)
        hit(3)
        spot(1)
        prod(3)
        spot(2)
        spot(3)
        op("t", "T16F " + names("RD"), "LS", "mm", T.LS[:, 16:48], V("T16F"), V("RD"), True, True)
        op("v", "LS GC", "RQ", "ts", T.RQ[:, :], T.LS[:, 16:48], col("GC"), 520.0, A.add, A.min)
        to_ranks("RQ", lambda i: T.RQ[:, 8 * i:8 * i + 8], lambda j: T.REQ[:, 8 * j:8 * j + 8], 0, "rar")
        x_to("XSN", near[1:], 4, 1)
        op("v", "MS " + names("MS") + " " + names("DD"), "PP", "tt", T.PP[:, :], T.MS[:, :], T.DD[:, :], A.mult)
        idt()
        for i in four:
            op("t", "IDT PP", "LS", "mm", T.LS[:, 128:256], V("IDT"), blk(T.PP, i, 1), i == 0, i == 3)
        op("v", "OW", "FA", "ts", V("FA"), V("OW"), float(r), -128.0, A.is_gt, A.mult)
        op("v", "OW", "FB", "ts", V("FB"), V("OW"), 128.0, 4095.0, A.mult, A.add)
        op("v", "NB", "VL", "ts", V("VL"), T.NB[:, :], 4095, None, A.bitwise_and)
        op("v", "FA FB", "FC", "tt", V("FC"), V("FA"), V("FB"), A.add)
        op("v", "OW", "RM", "ts", V("RM"), V("OW"), float(r), None, A.not_equal)
        op("v", "FC VL", "FE", "tt", V("FE"), V("FC"), V("VL"), A.subtract)
        op("v", "FE LS", "FD", "tt", V("FD"), V("FE"), T.LS[:, 128:256], A.add)
        op("v", "FD RM", "FF", "tt", V("FF"), V("FD"), V("RM"), A.mult)
        op("v", "FF VL", "FG", "tt", V("FG"), V("FF"), V("VL"), A.add)
        op("v", "FG", "OFF", "copy", T.OFF[:, :], V("FG"))
        to_team("REQ", T.REQ[:, :], "far")
        to_team("OFF", T.OFF[:, :], "oar")
        matrices([0], 256)
        pads(0)

    OPB = ("OP", "PC", "OP")

    def own(k):
        return names("OWN%d_" % k, 5)

    def request(k):
        win = T["OWN%d" % k][:, 0:528]
        rk = "REQ ZA%d ZZ%d " % (k, k) + own(k)
        op("v", rk, "GS0", "copy", T.GS[:, 0:256], win.indirect(T.REQ[:, 0:16]))
        op("s", rk, "GS1", "act", T.GS[:, 256:512], win.indirect(T.REQ[:, 16:32]), COPY)
        for a in range(8):
            op("t", "GS0 GS1 BLK%d" % a, "PH", "mm", T.PH[:, 0:64], blkm(a), T.GS[:, a:512:8], a == 0, a == 7)
        hs, hl = "HS%d" % k, "HL%d" % k
        op("v", "PH", hs, "copy", T[hs][:, :], T.PH[:, 0:64])
        to_ranks(hs, lambda i: T[hs][:, 16 * i:16 * i + 16], lambda j: T[hl][:, 16 * j:16 * j + 16], me, "h%d" % k)

    def spread(k, a, lo, hi, keys):
        b = "R%d" % (a % 4)
        op("t", keys + " SEL%d" % a, b, "mm", T[b][:, lo:hi], sel(a), T["OWN%d" % k][:, 8 + lo:8 + hi], True, True)

    def own_psum(k, lo, hi, keys):
        op("t", keys + " IDT", OPB[k], "mm", T[OPB[k]][:, lo:hi], V("IDT"), T["OWN%d" % k][:, 8 + lo:8 + hi], True, True)

    def replicate(k):
        if k:
            own_psum(k, HALF, 512, own(k))
        for a in range(8):
            b = "R%d" % (a % 4)
            spread(k, a, HALF if k and a < 4 else 0, 512, own(k))
            out = T.WIN[:, 512 * a:512 * a + 512]
            if a % 2:
                op("s", b, "WIN%d" % a, "act", out, T[b][:, :], COPY)
            else:
                op("v", b, "WIN%d" % a, "copy", out, T[b][:, :])

    def sweep(k):
        h = "HL%d" % k
        for b, p in (("PH", 0), ("LS", 1)):
            for a in range(p, 8, 2):
                op("t", h + " SEL%d" % a, b, "mm", T[b][:, a // 2:256:4], sel(a), T[h][:, :], True, True)
        op("v", "PH", "WIN8", "copy", T.WIN[:, 4096:4608:2], T.PH[:, 0:256])
        op("s", "LS", "WIN9", "act", T.WIN[:, 4097:4608:2], T.LS[:, 0:256], COPY)
        out, o8 = (T["OWN%d" % (k + 1)], 8) if k < 2 else (T.Y, 0)
        dst = own(k + 1).split() if k < 2 else names("Y", 5).split()
        for i, (a, b) in enumerate(CUT):
            nbr = T.WIN[:, 0:4608].indirect(T.OFF[:, a // 4:b // 4])
            if i == 0:
                op("v", "OFF " + names("WIN", 10), "GA0", "copy", T.GA[:, 4 * a:4 * b], nbr)
            else:
                op("s", "OFF " + names("WIN", 10), "GA%d" % i, "act", T.GA[:, 4 * a:4 * b], nbr, COPY)

        def scan(i):
            a, b = CUT[i]
            op("v", "GA%d MK" % i, "SC%d" % i, "scan", T.SC[:, 4 * a:4 * b], T.MK[:, 0:4 * (b - a)], T.GA[:, 4 * a:4 * b],
               0.0, A.min, A.max)

        def final(i):
            a, b = CUT[i]
            op("v", OPB[k] + " SC%d" % i, dst[i], "tt", out[:, o8 + a:o8 + b], T.SC[:, 4 * a + 3:4 * b:4], T[OPB[k]][:, a:b],
               A.max)
        for f, i in ((scan, 0), (scan, 1), (final, 0), (final, 1), (scan, 2), (final, 2), (scan, 3), (final, 3), (scan, 4),
                     (final, 4)):
            f(i)
        if k < 2:
            for a in four:
                spread(k + 1, a, 0, HALF, " ".join(dst[0:3]))
            own_psum(k + 1, 0, HALF, " ".join(dst[0:3]))

    op("t", "XL PRM", "R0", "mm", T.R0[:, 0:256], V("PRM"), T.XL[:, 0:256], True, True)
    op("t", "XL PRM", "R1", "mm", T.R1[:, 0:256], V("PRM"), T.XL[:, 256:512], True, True)
    op("t", "XL PRM", "OP", "mm", T.OP[:, :], V("PRM"), T.XL[:, :], True, True)
    if first:
        op("s", "R0", "OWN0_0 OWN0_1", "act", T.OWN0[:, 8:264], T.R0[:, 0:256], COPY)
    else:
        op("v", "R0", "OWN0_0 OWN0_1", "copy", T.OWN0[:, 8:264], T.R0[:, 0:256])
    op("s", "R1", "OWN0_2 OWN0_3 OWN0_4", "act", T.OWN0[:, 264:520], T.R1[:, 0:256], COPY)
    for k in range(3):
        request(k)
        if k == 0 and first:
            for_sweep()
        replicate(k)
        sweep(k)

    for h, ks, lo, hi in (("A", "Y0 Y1 Y2", 0, HALF), ("B", "Y3 Y4", HALF, 512)):
        yd, s = T["YD" + h], h.lower()
        if first:
            for k in range(8):
                dma("y" if h == "A" else "ys"[k % 2], ks, "y", "yo", T.y[0:16, 512 * k + lo:512 * k + hi],
                    T.Y[16 * k:16 * k + 16, lo:hi], 512)
            for k in range(8):
                dma("ys"[k % 2], "YR" + h, "y", "yo", T.y[16:128, 512 * k + lo:512 * k + hi],
                    yd[1:8, 16 * k:16 * k + 16, :], 512)
        else:
            e = engines(team[r][0])
            send(ks, [transfer(team[r][0], T.Y[:, lo:hi], yd[me], e, "yr" + s)], len(e))
    finish()
